import numpy as np
CORES = [32,33,34,35,36,37,38,39,40,41,42,43,44,45,46,47,48,49,50,51,52,53,54,55,56,57,58,59,60,61,62,63]
N = 32
GROUPS = [[0,1,2,3,4,5,6,7],[8,9,10,11,12,13,14,15],[16,17,18,19,20,21,22,23],[24,25,26,27,28,29,30,31]]
def setup_inputs(rng):
    return {"x": rng.standard_normal((N, 128, 256), dtype=np.float32)}
def reference(x):
    y = np.empty((N, 128, 256), x.dtype)
    for g in GROUPS:
        s = x[g].sum(axis=0, dtype=np.float64).astype(x[g].dtype)
        for r in g:
            y[r] = s
    return {"y": y}

@@ -1,0 +1,54 @@
+from concourse.bass import DstId, RemoteDMATransfer
+
+SCRATCH = {
+    "xs": ("dram", [4, 128, 64], "float32"),
+    "land": ("dram", [8, 128, 64], "float32"),
+    "res": ("dram", [4, 128, 64], "float32"),
+}
+SEMAPHORES = ["loaded", "pieces", "sums", "sent", "stored"]
+
+
+def rank_program(g, core, T, topo):
+    if T.rank_of(core) is None:
+        return
+    base = core - core % 8
+    k = core % 8
+
+    def dst(c):
+        rid, pid, _se = topo.addr(c)
+        return DstId(rid=rid, pnc=pid)
+
+    g.sync.dma_start(T.xs[:], T.x[:]).then_inc(T.sem.loaded, 16)
+    g.wait_ge(T.sem.loaded, 16)
+
+    scatter = []
+    for q in range(4):
+        to = [c for c in (q, q + 4) if c != k]
+        scatter.append(RemoteDMATransfer(
+            dst_ids=[dst(base + c) for c in to],
+            dma_engine_mask=0xF << (4 * q),
+            remote_sem=T.sem.pieces,
+            srcs=[T.xs[q]],
+            dsts=[T.land[k] for _c in to],
+            alu_op=0,
+        ))
+    g.remote_dma_fused(scatter, local_sem=T.sem.sent)
+
+    g.wait_ge(T.sem.pieces, 7 * 4)
+    q = k % 4
+    die0 = k - q
+    to = [die0 + c for c in range(4) if c != q] + [k ^ 4]
+    srcs = [T.xs[q] if s == k else T.land[s] for s in range(8)]
+    g.remote_dma_fused([RemoteDMATransfer(
+        dst_ids=[dst(base + c) for c in to],
+        dma_engine_mask=0xFFFF,
+        remote_sem=T.sem.sums,
+        srcs=srcs,
+        dsts=[T.res[q] for _c in to],
+        alu_op=1,
+    )], local_sem=T.sem.sent)
+
+    g.sync.wait_ge(T.sem.sums, 4 * 16)
+    g.sync.dma_start(T.y[:], T.res[:]).then_inc(T.sem.stored, 16)
+    g.wait_ge(T.sem.sent, 32)
+    g.sync.wait_ge(T.sem.stored, 16)

@@ -1,11 +1,11 @@
 from concourse.bass import DstId, RemoteDMATransfer
 
 SCRATCH = {
-    "xs": ("dram", [4, 128, 64], "float32"),
-    "land": ("dram", [8, 128, 64], "float32"),
-    "res": ("dram", [4, 128, 64], "float32"),
+    "xs": ("dram", [8, 128, 32], "float32"),
+    "land": ("dram", [16, 128, 32], "float32"),
+    "res": ("dram", [8, 128, 32], "float32"),
 }
-SEMAPHORES = ["loaded", "pieces", "sums", "sent", "stored"]
+SEMAPHORES = ["loaded0", "loaded1", "pieces0", "pieces1", "sums0", "sums1", "sent", "stored0", "stored1"]
 
 
 def rank_program(g, core, T, topo):
@@ -13,42 +13,46 @@ def rank_program(g, core, T, topo):
         return
     base = core - core % 8
     k = core % 8
+    queue = (g.sync, g.scalar)
 
     def dst(c):
         rid, pid, _se = topo.addr(c)
         return DstId(rid=rid, pnc=pid)
 
-    g.sync.dma_start(T.xs[:], T.x[:]).then_inc(T.sem.loaded, 16)
-    g.wait_ge(T.sem.loaded, 16)
+    for h in range(2):
+        queue[h].dma_start(T.xs[4 * h:4 * h + 4], T.x[64 * h:64 * h + 64, :]).then_inc(T.sem["loaded%d" % h], 16)
 
-    scatter = []
-    for q in range(4):
-        to = [c for c in (q, q + 4) if c != k]
-        scatter.append(RemoteDMATransfer(
-            dst_ids=[dst(base + c) for c in to],
-            dma_engine_mask=0xF << (4 * q),
-            remote_sem=T.sem.pieces,
-            srcs=[T.xs[q]],
-            dsts=[T.land[k] for _c in to],
-            alu_op=0,
-        ))
-    g.remote_dma_fused(scatter, local_sem=T.sem.sent)
+    for h in range(2):
+        g.wait_ge(T.sem["loaded%d" % h], 16)
+        scatter = []
+        for q in range(4):
+            to = [c for c in (q, q + 4) if c != k]
+            scatter.append(RemoteDMATransfer(
+                dst_ids=[dst(base + c) for c in to],
+                dma_engine_mask=0xF << (4 * q),
+                remote_sem=T.sem["pieces%d" % h],
+                srcs=[T.xs[4 * h + q]],
+                dsts=[T.land[8 * h + k] for _c in to],
+                alu_op=0,
+            ))
+        g.remote_dma_fused(scatter, local_sem=T.sem.sent)
 
-    g.wait_ge(T.sem.pieces, 7 * 4)
     q = k % 4
-    die0 = k - q
-    to = [die0 + c for c in range(4) if c != q] + [k ^ 4]
-    srcs = [T.xs[q] if s == k else T.land[s] for s in range(8)]
-    g.remote_dma_fused([RemoteDMATransfer(
-        dst_ids=[dst(base + c) for c in to],
-        dma_engine_mask=0xFFFF,
-        remote_sem=T.sem.sums,
-        srcs=srcs,
-        dsts=[T.res[q] for _c in to],
-        alu_op=1,
-    )], local_sem=T.sem.sent)
+    to = [k - q + c for c in range(4) if c != q] + [k ^ 4]
+    for h in range(2):
+        g.wait_ge(T.sem["pieces%d" % h], 7 * 4)
+        g.remote_dma_fused([RemoteDMATransfer(
+            dst_ids=[dst(base + c) for c in to],
+            dma_engine_mask=0xFFFF,
+            remote_sem=T.sem["sums%d" % h],
+            srcs=[T.xs[4 * h + q] if s == k else T.land[8 * h + s] for s in range(8)],
+            dsts=[T.res[4 * h + q] for _c in to],
+            alu_op=1,
+        )], local_sem=T.sem.sent)
 
-    g.sync.wait_ge(T.sem.sums, 4 * 16)
-    g.sync.dma_start(T.y[:], T.res[:]).then_inc(T.sem.stored, 16)
-    g.wait_ge(T.sem.sent, 32)
-    g.sync.wait_ge(T.sem.stored, 16)
+    for h in range(2):
+        queue[h].wait_ge(T.sem["sums%d" % h], 4 * 16)
+        queue[h].dma_start(T.y[64 * h:64 * h + 64, :], T.res[4 * h:4 * h + 4]).then_inc(T.sem["stored%d" % h], 16)
+    g.wait_ge(T.sem.sent, 64)
+    for h in range(2):
+        queue[h].wait_ge(T.sem["stored%d" % h], 16)

from concourse.bass import DstId, RemoteDMATransfer

SCRATCH = {
    "xs": ("dram", [8, 128, 32], "float32"),
    "land": ("dram", [16, 128, 32], "float32"),
    "res": ("dram", [8, 128, 32], "float32"),
}
SEMAPHORES = ["loaded0", "loaded1", "pieces0", "pieces1", "sums0", "sums1", "sent", "stored0", "stored1"]


def rank_program(g, core, T, topo):
    if T.rank_of(core) is None:
        return
    base = core - core % 8
    k = core % 8
    queue = (g.sync, g.scalar)

    def dst(c):
        rid, pid, _se = topo.addr(c)
        return DstId(rid=rid, pnc=pid)

    for h in range(2):
        queue[h].dma_start(T.xs[4 * h:4 * h + 4], T.x[64 * h:64 * h + 64, :]).then_inc(T.sem["loaded%d" % h], 16)

    for h in range(2):
        g.wait_ge(T.sem["loaded%d" % h], 16)
        scatter = []
        for q in range(4):
            to = [c for c in (q, q + 4) if c != k]
            scatter.append(RemoteDMATransfer(
                dst_ids=[dst(base + c) for c in to],
                dma_engine_mask=0xF << (4 * q),
                remote_sem=T.sem["pieces%d" % h],
                srcs=[T.xs[4 * h + q]],
                dsts=[T.land[8 * h + k] for _c in to],
                alu_op=0,
            ))
        g.remote_dma_fused(scatter, local_sem=T.sem.sent)

    q = k % 4
    to = [k - q + c for c in range(4) if c != q] + [k ^ 4]
    for h in range(2):
        g.wait_ge(T.sem["pieces%d" % h], 7 * 4)
        g.remote_dma_fused([RemoteDMATransfer(
            dst_ids=[dst(base + c) for c in to],
            dma_engine_mask=0xFFFF,
            remote_sem=T.sem["sums%d" % h],
            srcs=[T.xs[4 * h + q] if s == k else T.land[8 * h + s] for s in range(8)],
            dsts=[T.res[4 * h + q] for _c in to],
            alu_op=1,
        )], local_sem=T.sem.sent)

    for h in range(2):
        queue[h].wait_ge(T.sem["sums%d" % h], 4 * 16)
        queue[h].dma_start(T.y[64 * h:64 * h + 64, :], T.res[4 * h:4 * h + 4]).then_inc(T.sem["stored%d" % h], 16)
    g.wait_ge(T.sem.sent, 64)
    for h in range(2):
        queue[h].wait_ge(T.sem["stored%d" % h], 16)
